import numpy as np
import ml_dtypes

BF16 = ml_dtypes.bfloat16


def bf(x):
    return np.asarray(x, np.float32).astype(BF16)


def f32(x):
    return np.asarray(x, np.float32)


def f64(x):
    return np.asarray(x).astype(np.float64)


def striped(idx):
    return np.concatenate([l.reshape(-1, 16).T for l in idx])


def rows(idx, k):
    return np.tile(np.repeat(idx, 16, axis=0), (k // (16 * 8), 1))


def look(tab, idx):
    return np.take_along_axis(f64(tab), rows(idx, len(tab)), axis=1)


K, S, D, V, N = 128, 2048, 2, 1024, 2048


def setup_inputs():
    return {"tab": f32(np.random.standard_normal((K, S))), "ctr": f32(1.0 * np.random.standard_normal((K, V))), "offs": striped(np.stack([np.random.permutation(S)[:N] for _ in range(8)]))}


def reference(tab, ctr, offs):
    idx = np.stack([g.T.reshape(-1) for g in np.split(offs, 8)])
    e = [np.abs(look(tab, idx[:, d * V:(d + 1) * V]) - f64(ctr)) for d in range(D)]
    x = sum(np.minimum(v, 1.0) * (v - 0.5 * np.minimum(v, 1.0)) for v in e)
    return x

@@ -1,0 +1,54 @@
+import math
+
+import concourse.mybir as mybir
+
+F32, U16 = mybir.dt.float32, mybir.dt.uint16
+ADD, SUB = mybir.AluOpType.add, mybir.AluOpType.subtract
+MAX, MIN = mybir.AluOpType.max, mybir.AluOpType.min
+ABS = mybir.ActivationFunctionType.Abs
+RELU = mybir.ActivationFunctionType.Relu
+SQUARE = mybir.ActivationFunctionType.Square
+
+P = 128
+S = 2048
+D = 2
+V = 1024
+N = D * V
+PIECE = 512
+
+
+def tile_lookup_huber_out_kernel(tc, tab, ctr, offs, out):
+    nc = tc.nc
+    with tc.tile_pool(name="held", bufs=1) as held:
+        offsets = held.tile([P, N // 16], U16, name="offsets")
+        table = held.tile([P, S], F32, name="table")
+        target = held.tile([P, V], F32, name="target")
+        nc.sync.dma_start(offsets[:], offs)
+        nc.sync.dma_start(table[:], tab)
+        nc.sync.dma_start(target[:], ctr)
+
+        for first in range(0, V, PIECE):
+            cols = slice(first, first + PIECE)
+            losses = []
+            for d in range(D):
+                entry = d * V + first
+                picks = offsets[:, entry // 16:(entry + PIECE) // 16]
+                diff = held.tile([P, PIECE], F32, name=f"diff_{first}_{d}")
+                nc.vector.tensor_tensor(diff[:], table[:].indirect(picks), target[:, cols], SUB)
+
+                clamped = held.tile([P, PIECE], F32, name=f"clamped_{first}_{d}")
+                nc.vector.tensor_scalar(clamped[:], diff[:], -1.0, 1.0, MAX, MIN)
+                size = held.tile([P, PIECE], F32, name=f"size_{first}_{d}")
+                nc.scalar.activation(size[:], diff[:], ABS)
+                linear = held.tile([P, PIECE], F32, name=f"linear_{first}_{d}")
+                nc.scalar.activation(linear[:], size[:], RELU, bias=-1.0)
+                squared = held.tile([P, PIECE], F32, name=f"squared_{first}_{d}")
+                nc.scalar.activation(squared[:], clamped[:], SQUARE, scale=math.sqrt(0.5))
+
+                loss = held.tile([P, PIECE], F32, name=f"loss_{first}_{d}")
+                nc.vector.tensor_tensor(loss[:], squared[:], linear[:], ADD)
+                losses.append(loss)
+
+            total = held.tile([P, PIECE], F32, name=f"total_{first}")
+            nc.vector.tensor_tensor(total[:], losses[0][:], losses[1][:], ADD)
+            nc.sync.dma_start(out[:, cols], total[:])

@@ -19,36 +19,49 @@ PIECE = 512
 
 def tile_lookup_huber_out_kernel(tc, tab, ctr, offs, out):
     nc = tc.nc
+    blocks = range(0, V, PIECE)
     with tc.tile_pool(name="held", bufs=1) as held:
         offsets = held.tile([P, N // 16], U16, name="offsets")
         table = held.tile([P, S], F32, name="table")
-        target = held.tile([P, V], F32, name="target")
         nc.sync.dma_start(offsets[:], offs)
         nc.sync.dma_start(table[:], tab)
-        nc.sync.dma_start(target[:], ctr)
+        targets = {}
+        for first in blocks:
+            targets[first] = held.tile([P, PIECE], F32, name=f"target_{first}")
+            nc.sync.dma_start(targets[first][:], ctr[:, first:first + PIECE])
 
-        for first in range(0, V, PIECE):
-            cols = slice(first, first + PIECE)
-            losses = []
-            for d in range(D):
-                entry = d * V + first
-                picks = offsets[:, entry // 16:(entry + PIECE) // 16]
-                diff = held.tile([P, PIECE], F32, name=f"diff_{first}_{d}")
-                nc.vector.tensor_tensor(diff[:], table[:].indirect(picks), target[:, cols], SUB)
+        def look_up(first, d):
+            entry = d * V + first
+            picks = offsets[:, entry // 16:(entry + PIECE) // 16]
+            diff = held.tile([P, PIECE], F32, name=f"diff_{first}_{d}")
+            nc.vector.tensor_tensor(diff[:], table[:].indirect(picks), targets[first][:], SUB)
+            size = held.tile([P, PIECE], F32, name=f"size_{first}_{d}")
+            nc.scalar.activation(size[:], diff[:], ABS)
+            linear = held.tile([P, PIECE], F32, name=f"linear_{first}_{d}")
+            nc.scalar.activation(linear[:], size[:], RELU, bias=-1.0)
+            return diff, linear
 
-                clamped = held.tile([P, PIECE], F32, name=f"clamped_{first}_{d}")
-                nc.vector.tensor_scalar(clamped[:], diff[:], -1.0, 1.0, MAX, MIN)
-                size = held.tile([P, PIECE], F32, name=f"size_{first}_{d}")
-                nc.scalar.activation(size[:], diff[:], ABS)
-                linear = held.tile([P, PIECE], F32, name=f"linear_{first}_{d}")
-                nc.scalar.activation(linear[:], size[:], RELU, bias=-1.0)
-                squared = held.tile([P, PIECE], F32, name=f"squared_{first}_{d}")
-                nc.scalar.activation(squared[:], clamped[:], SQUARE, scale=math.sqrt(0.5))
+        def half_square(first, d, diff):
+            clamped = held.tile([P, PIECE], F32, name=f"clamped_{first}_{d}")
+            nc.vector.tensor_scalar(clamped[:], diff[:], -1.0, 1.0, MAX, MIN)
+            squared = held.tile([P, PIECE], F32, name=f"squared_{first}_{d}")
+            nc.scalar.activation(squared[:], clamped[:], SQUARE, scale=math.sqrt(0.5))
+            return squared
 
-                loss = held.tile([P, PIECE], F32, name=f"loss_{first}_{d}")
-                nc.vector.tensor_tensor(loss[:], squared[:], linear[:], ADD)
-                losses.append(loss)
+        pieces = [(first, d) for first in blocks for d in range(D)]
+        diffs, linear, squared = {}, {}, {}
+        for i, piece in enumerate(pieces):
+            diffs[piece], linear[piece] = look_up(*piece)
+            if i > 0:
+                before = pieces[i - 1]
+                squared[before] = half_square(*before, diffs[before])
+        squared[piece] = half_square(*piece, diffs[piece])
 
+        loss = {}
+        for first, d in pieces:
+            loss[first, d] = held.tile([P, PIECE], F32, name=f"loss_{first}_{d}")
+            nc.vector.tensor_tensor(loss[first, d][:], squared[first, d][:], linear[first, d][:], ADD)
+        for first in blocks:
             total = held.tile([P, PIECE], F32, name=f"total_{first}")
-            nc.vector.tensor_tensor(total[:], losses[0][:], losses[1][:], ADD)
-            nc.sync.dma_start(out[:, cols], total[:])
+            nc.vector.tensor_tensor(total[:], loss[first, 0][:], loss[first, 1][:], ADD)
+            nc.sync.dma_start(out[:, first:first + PIECE], total[:])

@@ -57,11 +57,16 @@ def tile_lookup_huber_out_kernel(tc, tab, ctr, offs, out):
                 squared[before] = half_square(*before, diffs[before])
         squared[piece] = half_square(*piece, diffs[piece])
 
-        loss = {}
-        for first, d in pieces:
-            loss[first, d] = held.tile([P, PIECE], F32, name=f"loss_{first}_{d}")
-            nc.vector.tensor_tensor(loss[first, d][:], squared[first, d][:], linear[first, d][:], ADD)
-        for first in blocks:
-            total = held.tile([P, PIECE], F32, name=f"total_{first}")
-            nc.vector.tensor_tensor(total[:], loss[first, 0][:], loss[first, 1][:], ADD)
-            nc.sync.dma_start(out[:, first:first + PIECE], total[:])
+        def plus(a, b, name):
+            total = held.tile([P, PIECE], F32, name=name)
+            nc.vector.tensor_tensor(total[:], a[:], b[:], ADD)
+            return total
+
+        early, late = blocks
+        losses = [plus(linear[early, d], squared[early, d], f"loss_{d}") for d in range(D)]
+        late_sum = plus(linear[late, 0], linear[late, 1], "late_linear")
+        early_total = plus(losses[0], losses[1], "early_total")
+        nc.sync.dma_start(out[:, early:early + PIECE], early_total[:])
+        late_sum = plus(late_sum, squared[late, 0], "late_but_one")
+        late_total = plus(late_sum, squared[late, 1], "late_total")
+        nc.sync.dma_start(out[:, late:late + PIECE], late_total[:])

@@ -63,10 +63,10 @@ def tile_lookup_huber_out_kernel(tc, tab, ctr, offs, out):
             return total
 
         early, late = blocks
-        losses = [plus(linear[early, d], squared[early, d], f"loss_{d}") for d in range(D)]
-        late_sum = plus(linear[late, 0], linear[late, 1], "late_linear")
+        losses = [plus(linear[early, d], squared[early, d], f"early_{d}") for d in range(D)]
+        late_sum = plus(linear[late, 0], squared[late, 0], "late_0")
         early_total = plus(losses[0], losses[1], "early_total")
         nc.sync.dma_start(out[:, early:early + PIECE], early_total[:])
-        late_sum = plus(late_sum, squared[late, 0], "late_but_one")
+        late_sum = plus(late_sum, linear[late, 1], "late_but_one")
         late_total = plus(late_sum, squared[late, 1], "late_total")
         nc.sync.dma_start(out[:, late:late + PIECE], late_total[:])

import math

import concourse.mybir as mybir

F32, U16 = mybir.dt.float32, mybir.dt.uint16
ADD, SUB = mybir.AluOpType.add, mybir.AluOpType.subtract
MAX, MIN = mybir.AluOpType.max, mybir.AluOpType.min
ABS = mybir.ActivationFunctionType.Abs
RELU = mybir.ActivationFunctionType.Relu
SQUARE = mybir.ActivationFunctionType.Square

P = 128
S = 2048
D = 2
V = 1024
N = D * V
PIECE = 512


def tile_lookup_huber_out_kernel(tc, tab, ctr, offs, out):
    nc = tc.nc
    blocks = range(0, V, PIECE)
    with tc.tile_pool(name="held", bufs=1) as held:
        offsets = held.tile([P, N // 16], U16, name="offsets")
        table = held.tile([P, S], F32, name="table")
        nc.sync.dma_start(offsets[:], offs)
        nc.sync.dma_start(table[:], tab)
        targets = {}
        for first in blocks:
            targets[first] = held.tile([P, PIECE], F32, name=f"target_{first}")
            nc.sync.dma_start(targets[first][:], ctr[:, first:first + PIECE])

        def look_up(first, d):
            entry = d * V + first
            picks = offsets[:, entry // 16:(entry + PIECE) // 16]
            diff = held.tile([P, PIECE], F32, name=f"diff_{first}_{d}")
            nc.vector.tensor_tensor(diff[:], table[:].indirect(picks), targets[first][:], SUB)
            size = held.tile([P, PIECE], F32, name=f"size_{first}_{d}")
            nc.scalar.activation(size[:], diff[:], ABS)
            linear = held.tile([P, PIECE], F32, name=f"linear_{first}_{d}")
            nc.scalar.activation(linear[:], size[:], RELU, bias=-1.0)
            return diff, linear

        def half_square(first, d, diff):
            clamped = held.tile([P, PIECE], F32, name=f"clamped_{first}_{d}")
            nc.vector.tensor_scalar(clamped[:], diff[:], -1.0, 1.0, MAX, MIN)
            squared = held.tile([P, PIECE], F32, name=f"squared_{first}_{d}")
            nc.scalar.activation(squared[:], clamped[:], SQUARE, scale=math.sqrt(0.5))
            return squared

        pieces = [(first, d) for first in blocks for d in range(D)]
        diffs, linear, squared = {}, {}, {}
        for i, piece in enumerate(pieces):
            diffs[piece], linear[piece] = look_up(*piece)
            if i > 0:
                before = pieces[i - 1]
                squared[before] = half_square(*before, diffs[before])
        squared[piece] = half_square(*piece, diffs[piece])

        def plus(a, b, name):
            total = held.tile([P, PIECE], F32, name=name)
            nc.vector.tensor_tensor(total[:], a[:], b[:], ADD)
            return total

        early, late = blocks
        losses = [plus(linear[early, d], squared[early, d], f"early_{d}") for d in range(D)]
        late_sum = plus(linear[late, 0], squared[late, 0], "late_0")
        early_total = plus(losses[0], losses[1], "early_total")
        nc.sync.dma_start(out[:, early:early + PIECE], early_total[:])
        late_sum = plus(late_sum, linear[late, 1], "late_but_one")
        late_total = plus(late_sum, squared[late, 1], "late_total")
        nc.sync.dma_start(out[:, late:late + PIECE], late_total[:])
